import numpy as np
import ml_dtypes


def mxq(x, axis, fmt="e4m3"):
    dtype, down = {"e4m3": (ml_dtypes.float8_e4m3fn, 7), "e5m2": (ml_dtypes.float8_e5m2, 14)}[fmt]
    v = np.moveaxis(np.asarray(x, np.float32).astype(ml_dtypes.bfloat16).astype(np.float64), axis, -1)
    blocks = v.reshape(v.shape[:-1] + (-1, 32))
    amax = np.abs(blocks).max(-1, keepdims=True)
    byte = np.maximum(np.where(amax > 0, np.frexp(amax)[1] - 1 + 127, 0) - down, 1)
    scale = np.exp2(byte - 127.0)
    codes = (blocks / scale).astype(np.float32).astype(dtype).astype(np.float64)
    return np.moveaxis((codes * scale).reshape(v.shape), -1, axis)


WIDE = False


def mx_kscale(k):
    if not WIDE:
        return np.ones(k)
    levels = np.array([10, -10, 5, -5, 0])
    if k % 512:
        return np.exp2(np.random.permutation(np.resize(levels, k // 32))).repeat(32)
    a = np.empty((k // 512, 16))
    for p in range(k // 512):
        a[p, :8] = np.random.permutation(np.resize(levels, 8))
        for g in range(8):
            far = levels[np.abs(levels - a[p, g]) >= 10]
            a[p, g + 8] = far[np.random.randint(len(far))]
    return np.exp2(a.ravel()).repeat(32)


def f64(x):
    return np.asarray(x).astype(np.float64)


def striped(idx):
    return np.tile(idx.reshape(-1, 16).T, (8, 1)).astype(np.uint16)


def unstriped(offs):
    return offs[:16].T.reshape(-1).astype(np.int64)

def planes(y):
    n, m = y.shape
    v = y.astype(np.float32).astype(ml_dtypes.bfloat16).astype(np.float64).reshape(n // 32, 32, m)
    top = np.abs(v).max(1)
    byte = np.clip(np.where(top > 0, np.frexp(top)[1] - 1 + 127 - 7, 1), 1, 254)
    codes = (v * np.exp2(127.0 - byte)[:, None, :]).reshape(n, m).astype(np.float32).astype(ml_dtypes.float8_e4m3fn).view(np.uint8)
    words = codes.reshape(n // 512, 128, 4, m).transpose(0, 1, 3, 2)
    return np.ascontiguousarray(words), np.ascontiguousarray(byte.astype(np.uint8).reshape(n // 512, 16, m))


K, T, S, V, N = 512, 1024, 512, 128, 512


def setup_inputs():
    n = np.random.standard_normal
    s = mx_kscale(K)[:, None]
    return {
        "xT": (n((K, T)) * s).astype(np.float32),
        "w1": (n((K, N)) / np.sqrt(K) / s).astype(np.float32),
        "offs": striped(np.random.permutation(T)[:S]),
    }


def reference(xT, w1, offs):
    xq = mxq(f64(xT)[:, unstriped(offs)], 0, "e4m3")
    e = np.exp(mxq(f64(w1), 0, "e4m3").T @ xq)
    out_0 = np.log(e[:, :V] + e[:, V:2 * V] + e[:, 2 * V:3 * V] + e[:, 3 * V:4 * V])
    return (out_0,) + planes(out_0)

@@ -1,0 +1,171 @@
+from contextlib import ExitStack
+
+import concourse.mybir as mybir
+
+K, T, S, V, N = 512, 1024, 512, 128, 512
+D = S // V
+FLOPS = 2 * K * S * N
+
+F32 = mybir.dt.float32
+BF16 = mybir.dt.bfloat16
+U32 = mybir.dt.uint32
+I32 = mybir.dt.int32
+U16 = mybir.dt.uint16
+U8 = mybir.dt.uint8
+FP8X4 = mybir.dt.float8_e4m3fn_x4
+ALU = mybir.AluOpType
+ACT = mybir.ActivationFunctionType
+AX = mybir.AxisListType
+
+P = 128
+PACK = 4
+
+
+def tile_picked_lsep_none_lo_kernel(tc, xT, w1, offs, out_0, out_1, out_2):
+    nc = tc.nc
+    with ExitStack() as ctx:
+        sb = ctx.enter_context(tc.tile_pool(name="sb", bufs=1))
+        psum = ctx.enter_context(tc.psum_pool(name="psum", bufs=1))
+
+        offsets = sb.tile([P, S // 16], U16, name="offsets")
+        warm = sb.tile([P, 8], F32, name="warm")
+        warm_out = sb.tile([P, 8], F32, name="warm_out")
+        nc.vector.memset(warm[:], 0.0)
+        nc.scalar.activation(warm_out[:], warm[:], ACT.Exp)
+
+        x_rows = xT.rearrange("(p j) t -> p j t", j=PACK)
+        w_rows = w1.rearrange("(p j) m -> p j m", j=PACK)
+        HT = T // 2
+        x_raw = {}
+        for a in range(2):
+            for h in range(2):
+                x_raw[a, h] = sb.tile([P, 2, HT], F32, name="x_raw%d%d" % (a, h))
+                nc.sync.dma_start(out=x_raw[a, h][:], in_=x_rows[:, 2 * a : 2 * a + 2, h * HT : (h + 1) * HT])
+                if (a, h) == (0, 0):
+                    nc.sync.dma_start(offsets[:], offs)
+        HN = N // 2
+        w_raw = []
+        for c in range(2):
+            w_raw.append(sb.tile([P, PACK, HN], F32, name="w_raw%d" % c))
+            nc.sync.dma_start(out=w_raw[c][:], in_=w_rows[:, :, c * HN : (c + 1) * HN])
+
+        pairs = [sb.tile([P, T], U32, name="pairs%d" % a, align_bytes=64) for a in range(2)]
+        picked = sb.tile([P, 2, S], U32, name="picked", align_bytes=64)
+
+        def cast_x(a, h, eng):
+            dst = pairs[a][:, h * HT : (h + 1) * HT].bitcast(BF16).rearrange("p (c e) -> p c e", e=2)
+            src = x_raw[a, h][:].rearrange("p e c -> p c e")
+            if eng == "v":
+                nc.vector.tensor_copy(out=dst, in_=src)
+            else:
+                nc.scalar.copy(out=dst, in_=src)
+
+        cast_x(0, 0, "v")
+        cast_x(0, 1, "v")
+        nc.vector.tensor_copy(picked[:, 0, :], pairs[0][:].indirect(offsets[:]))
+        cast_x(1, 0, "s")
+        cast_x(1, 1, "v")
+        HS = S // 2
+        for h in range(2):
+            nc.vector.tensor_copy(
+                picked[:, 1, h * HS : (h + 1) * HS],
+                pairs[1][:].indirect(offsets[:, h * HS // 16 : (h + 1) * HS // 16]),
+            )
+
+        w_grouped = sb.tile([P, PACK, P, PACK], BF16, name="w_grouped", align_bytes=64)
+        HM = P // 2
+        for c in range(2):
+            nc.scalar.copy(
+                out=w_grouped[:, :, c * HM : (c + 1) * HM, :].rearrange("p t m j -> p m j t"),
+                in_=w_raw[c][:].rearrange("p j (m t) -> p m j t", t=PACK),
+            )
+
+        x_grouped = [sb.tile([P, HS * PACK], BF16, name="x_grouped%d" % h, align_bytes=64) for h in range(2)]
+        x_codes = sb.tile([P, S], U32, name="x_codes", align_bytes=64)
+        x_scales = sb.tile([P, S], U8, name="x_scales", align_bytes=64)
+        for h in range(2):
+            nc.vector.tensor_copy(
+                out=x_grouped[h][:].bitcast(I32).rearrange("p (n a) -> p n a", a=2),
+                in_=picked[:, :, h * HS : (h + 1) * HS].bitcast(I32).rearrange("p a n -> p n a"),
+            )
+        for h in range(2):
+            nc.vector.quantize_mx(
+                out=x_codes[:, h * HS : (h + 1) * HS].bitcast(FP8X4),
+                scales=x_scales[:, h * HS : (h + 1) * HS],
+                in_=x_grouped[h][:],
+            )
+
+        w_codes = [sb.tile([P, P], U32, name="w_codes%d" % t, align_bytes=64) for t in range(PACK)]
+        w_scales = [sb.tile([P, P], U8, name="w_scales%d" % t, align_bytes=64) for t in range(PACK)]
+        banks = [psum.tile([P, S], F32, name="bank%d" % t) for t in range(PACK)]
+        for t in range(PACK):
+            nc.vector.quantize_mx(
+                out=w_codes[t][:].bitcast(FP8X4),
+                scales=w_scales[t][:],
+                in_=w_grouped[:, t, :, :].rearrange("p m j -> p (m j)"),
+            )
+            nc.tensor.matmul_mx(
+                out=banks[t][:],
+                lhsT=w_codes[t][:].bitcast(FP8X4),
+                lhsT_scale=w_scales[t][:],
+                rhs=x_codes[:].bitcast(FP8X4),
+                rhs_scale=x_scales[:],
+                start=True,
+                stop=True,
+            )
+
+        top = sb.tile([P, PACK, V], F32, name="top")
+        shifted = [sb.tile([P, V, D], F32, name="shifted%d" % t) for t in range(PACK)]
+        expd = [sb.tile([P, V, D], F32, name="expd%d" % t) for t in range(PACK)]
+        total = sb.tile([P, PACK, V], F32, name="total")
+        logs = sb.tile([P, PACK, V], F32, name="logs")
+        result = sb.tile([P, PACK, V], F32, name="result")
+        HV = V // 2
+        halves = [slice(0, HV), slice(HV, V)]
+
+        def by_place(t):
+            return banks[t][:].rearrange("p (d v) -> p v d", d=D)
+
+        def largest(t):
+            nc.vector.tensor_reduce(out=top[:, t, :], in_=by_place(t), axis=AX.X, op=ALU.max)
+
+        def shift(t, vs):
+            nc.vector.tensor_tensor(
+                out=shifted[t][:, vs, :],
+                in0=by_place(t)[:, vs, :],
+                in1=top[:, t, vs].unsqueeze(2).to_broadcast([P, vs.stop - vs.start, D]),
+                op=ALU.subtract,
+            )
+            nc.scalar.activation(expd[t][:, vs, :], shifted[t][:, vs, :], ACT.Exp)
+
+        largest(0)
+        for t in range(1, PACK):
+            largest(t)
+            shift(t - 1, slice(0, V))
+        for vs in halves:
+            shift(PACK - 1, vs)
+        for t in range(PACK):
+            nc.vector.tensor_reduce(out=total[:, t, :], in_=expd[t][:], axis=AX.X, op=ALU.add)
+        for vs in halves:
+            nc.scalar.activation(logs[:, :, vs], total[:, :, vs], ACT.Ln)
+        for vs in halves:
+            nc.vector.tensor_tensor(out=result[:, :, vs], in0=logs[:, :, vs], in1=top[:, :, vs], op=ALU.add)
+        nc.sync.dma_start(out=out_0.rearrange("(p t) v -> p t v", t=PACK), in_=result[:])
+
+        y_grouped = [sb.tile([P, HV * PACK], BF16, name="y_grouped%d" % h, align_bytes=64) for h in range(2)]
+        y_codes = sb.tile([P, V], U32, name="y_codes", align_bytes=64)
+        y_scales = sb.tile([P, V], U8, name="y_scales", align_bytes=64)
+        for h, vs in enumerate(halves):
+            nc.vector.tensor_copy(
+                out=y_grouped[h][:].rearrange("p (v t) -> p v t", t=PACK),
+                in_=result[:, :, vs].rearrange("p t v -> p v t"),
+            )
+        for h, vs in enumerate(halves):
+            nc.vector.quantize_mx(out=y_codes[:, vs].bitcast(FP8X4), scales=y_scales[:, vs], in_=y_grouped[h][:])
+        nc.scalar.dma_start(
+            out=out_1.rearrange("z l c r -> (z l) (c r)").bitcast(I32), in_=y_codes[:].bitcast(I32)
+        )
+        scale_rows = out_2.rearrange("z q c -> (z q) c").bitcast(I32)
+        for q in range(4):
+            eng = nc.sync if q % 2 == 0 else nc.scalar
+            eng.dma_start(out=scale_rows[4 * q : 4 * q + 4, :], in_=y_scales[32 * q : 32 * q + 4, :].bitcast(I32))

@@ -43,28 +43,28 @@ def tile_picked_lsep_none_lo_kernel(tc, xT, w1, offs, out_0, out_1, out_2):
                 nc.sync.dma_start(out=x_raw[a, h][:], in_=x_rows[:, 2 * a : 2 * a + 2, h * HT : (h + 1) * HT])
                 if (a, h) == (0, 0):
                     nc.sync.dma_start(offsets[:], offs)
-        HN = N // 2
+        w_cuts = [0, 128, 256, 384, 512]
         w_raw = []
-        for c in range(2):
-            w_raw.append(sb.tile([P, PACK, HN], F32, name="w_raw%d" % c))
-            nc.sync.dma_start(out=w_raw[c][:], in_=w_rows[:, :, c * HN : (c + 1) * HN])
+        for c in range(len(w_cuts) - 1):
+            w_raw.append(sb.tile([P, PACK, w_cuts[c + 1] - w_cuts[c]], F32, name="w_raw%d" % c))
+            nc.sync.dma_start(out=w_raw[c][:], in_=w_rows[:, :, w_cuts[c] : w_cuts[c + 1]])
 
         pairs = [sb.tile([P, T], U32, name="pairs%d" % a, align_bytes=64) for a in range(2)]
         picked = sb.tile([P, 2, S], U32, name="picked", align_bytes=64)
 
-        def cast_x(a, h, eng):
-            dst = pairs[a][:, h * HT : (h + 1) * HT].bitcast(BF16).rearrange("p (c e) -> p c e", e=2)
-            src = x_raw[a, h][:].rearrange("p e c -> p c e")
-            if eng == "v":
-                nc.vector.tensor_copy(out=dst, in_=src)
-            else:
-                nc.scalar.copy(out=dst, in_=src)
+        def cast_x(copy, a, h, lo, hi):
+            copy(
+                out=pairs[a][:, h * HT + lo : h * HT + hi].bitcast(BF16).rearrange("p (c e) -> p c e", e=2),
+                in_=x_raw[a, h][:, :, lo:hi].rearrange("p e c -> p c e"),
+            )
 
-        cast_x(0, 0, "v")
-        cast_x(0, 1, "v")
+        X_SCALAR = 160
+        cast_x(nc.vector.tensor_copy, 0, 0, 0, HT)
+        cast_x(nc.vector.tensor_copy, 0, 1, 0, HT)
         nc.vector.tensor_copy(picked[:, 0, :], pairs[0][:].indirect(offsets[:]))
-        cast_x(1, 0, "s")
-        cast_x(1, 1, "v")
+        cast_x(nc.scalar.copy, 1, 0, 0, HT)
+        cast_x(nc.scalar.copy, 1, 1, 0, X_SCALAR)
+        cast_x(nc.vector.tensor_copy, 1, 1, X_SCALAR, HT)
         HS = S // 2
         for h in range(2):
             nc.vector.tensor_copy(
@@ -73,10 +73,9 @@ def tile_picked_lsep_none_lo_kernel(tc, xT, w1, offs, out_0, out_1, out_2):
             )
 
         w_grouped = sb.tile([P, PACK, P, PACK], BF16, name="w_grouped", align_bytes=64)
-        HM = P // 2
-        for c in range(2):
+        for c in range(len(w_raw)):
             nc.scalar.copy(
-                out=w_grouped[:, :, c * HM : (c + 1) * HM, :].rearrange("p t m j -> p m j t"),
+                out=w_grouped[:, :, w_cuts[c] // PACK : w_cuts[c + 1] // PACK, :].rearrange("p t m j -> p m j t"),
                 in_=w_raw[c][:].rearrange("p j (m t) -> p m j t", t=PACK),
             )
 
@@ -116,7 +115,7 @@ def tile_picked_lsep_none_lo_kernel(tc, xT, w1, offs, out_0, out_1, out_2):
 
         top = sb.tile([P, PACK, V], F32, name="top")
         shifted = [sb.tile([P, V, D], F32, name="shifted%d" % t) for t in range(PACK)]
-        expd = [sb.tile([P, V, D], F32, name="expd%d" % t) for t in range(PACK)]
+        expd = {t: sb.tile([P, V, D], F32, name="expd%d" % t) for t in range(1, PACK)}
         total = sb.tile([P, PACK, V], F32, name="total")
         logs = sb.tile([P, PACK, V], F32, name="logs")
         result = sb.tile([P, PACK, V], F32, name="result")
@@ -138,13 +137,29 @@ def tile_picked_lsep_none_lo_kernel(tc, xT, w1, offs, out_0, out_1, out_2):
             )
             nc.scalar.activation(expd[t][:, vs, :], shifted[t][:, vs, :], ACT.Exp)
 
+        spilled = [sb.tile([P, HV, D], F32, name="spilled%d" % h) for h in range(2)]
+        expd_first = [sb.tile([P, HV, D], F32, name="expd_first")[:], shifted[1][:, halves[1], :]]
         largest(0)
-        for t in range(1, PACK):
-            largest(t)
-            shift(t - 1, slice(0, V))
+        for h, vs in enumerate(halves):
+            nc.scalar.copy(out=spilled[h][:], in_=by_place(0)[:, vs, :])
+            nc.gpsimd.tensor_tensor(
+                out=shifted[0][:, vs, :],
+                in0=spilled[h][:],
+                in1=top[:, 0, vs].unsqueeze(2).to_broadcast([P, HV, D]),
+                op=ALU.subtract,
+            )
+        largest(1)
+        largest(2)
+        nc.scalar.activation(expd_first[0], shifted[0][:, halves[0], :], ACT.Exp)
+        shift(1, slice(0, V))
+        largest(3)
+        nc.scalar.activation(expd_first[1], shifted[0][:, halves[1], :], ACT.Exp)
+        shift(2, slice(0, V))
         for vs in halves:
             shift(PACK - 1, vs)
-        for t in range(PACK):
+        for h, vs in enumerate(halves):
+            nc.vector.tensor_reduce(out=total[:, 0, vs], in_=expd_first[h], axis=AX.X, op=ALU.add)
+        for t in range(1, PACK):
             nc.vector.tensor_reduce(out=total[:, t, :], in_=expd[t][:], axis=AX.X, op=ALU.add)
         for vs in halves:
             nc.scalar.activation(logs[:, :, vs], total[:, :, vs], ACT.Ln)

@@ -113,56 +113,70 @@ def tile_picked_lsep_none_lo_kernel(tc, xT, w1, offs, out_0, out_1, out_2):
                 stop=True,
             )
 
-        top = sb.tile([P, PACK, V], F32, name="top")
-        shifted = [sb.tile([P, V, D], F32, name="shifted%d" % t) for t in range(PACK)]
-        expd = {t: sb.tile([P, V, D], F32, name="expd%d" % t) for t in range(1, PACK)}
-        total = sb.tile([P, PACK, V], F32, name="total")
-        logs = sb.tile([P, PACK, V], F32, name="logs")
-        result = sb.tile([P, PACK, V], F32, name="result")
         HV = V // 2
         halves = [slice(0, HV), slice(HV, V)]
+        both = slice(0, 2)
+        top = sb.tile([P, PACK, V], F32, name="top")
+        logs = sb.tile([P, PACK, V], F32, name="logs")
+        result = sb.tile([P, PACK, V], F32, name="result")
+        expd = sb.tile([P, 2, PACK + 1, D * HV], F32, name="expd")
+        shifted = {t: sb.tile([P, 2, D * HV], F32, name="shifted%d" % t)[:] for t in (0, 2, 3)}
+        shifted[1] = expd[:].rearrange("p h s n -> p (h s) n")[:, PACK : PACK + 2, :]
 
-        def by_place(t):
-            return banks[t][:].rearrange("p (d v) -> p v d", d=D)
+        def scores(t, hs):
+            return banks[t][:].rearrange("p (d h v) -> p h d v", d=D, h=2)[:, hs, :, :]
 
-        def largest(t):
-            nc.vector.tensor_reduce(out=top[:, t, :], in_=by_place(t), axis=AX.X, op=ALU.max)
+        def largest(t, vs):
+            nc.vector.tensor_reduce(
+                out=top[:, t, vs],
+                in_=banks[t][:].rearrange("p (d v) -> p v d", d=D)[:, vs, :],
+                axis=AX.X,
+                op=ALU.max,
+            )
 
-        def shift(t, vs):
+        def shift(eng, src, t, hs):
+            tops = top[:, t, :].rearrange("p (h v) -> p h v", h=2)[:, hs, :]
+            eng.tensor_tensor(
+                out=shifted[t][:, hs, :].rearrange("p h (d v) -> p h d v", d=D),
+                in0=src,
+                in1=tops.unsqueeze(2).to_broadcast([P, hs.stop - hs.start, D, HV]),
+                op=ALU.subtract,
+            )
+
+        def exp(t, hs):
+            nc.scalar.activation(expd[:, hs, t, :], shifted[t][:, hs, :], ACT.Exp)
+
+        one = [slice(0, 1), slice(1, 2)]
+        largest(0, slice(0, V))
+        for h, hs in enumerate(one):
+            spilled = sb.tile([P, 1, D, HV], F32, name="spilled%d" % h)
+            nc.scalar.copy(out=spilled[:], in_=scores(0, hs))
+            shift(nc.gpsimd, spilled[:], 0, hs)
+        largest(1, slice(0, V))
+        largest(2, slice(0, V))
+        exp(0, one[0])
+        for t in (1, 2):
+            shift(nc.vector, scores(t, both), t, both)
+            exp(t, both)
+        exp(0, one[1])
+        for vs in halves:
+            largest(3, vs)
+        for hs in one:
+            shift(nc.vector, scores(3, hs), 3, hs)
+            exp(3, hs)
+
+        pair_sums = sb.tile([P, 2, PACK, 2 * HV], F32, name="pair_sums")
+        total = sb.tile([P, 2, PACK, HV], F32, name="total")
+        for hs, ts in ((both, slice(0, PACK - 1)), (one[0], slice(PACK - 1, PACK)), (one[1], slice(PACK - 1, PACK))):
             nc.vector.tensor_tensor(
-                out=shifted[t][:, vs, :],
-                in0=by_place(t)[:, vs, :],
-                in1=top[:, t, vs].unsqueeze(2).to_broadcast([P, vs.stop - vs.start, D]),
-                op=ALU.subtract,
+                out=pair_sums[:, hs, ts, :], in0=expd[:, hs, ts, 0 : 2 * HV], in1=expd[:, hs, ts, 2 * HV : 4 * HV], op=ALU.add
             )
-            nc.scalar.activation(expd[t][:, vs, :], shifted[t][:, vs, :], ACT.Exp)
-
-        spilled = [sb.tile([P, HV, D], F32, name="spilled%d" % h) for h in range(2)]
-        expd_first = [sb.tile([P, HV, D], F32, name="expd_first")[:], shifted[1][:, halves[1], :]]
-        largest(0)
-        for h, vs in enumerate(halves):
-            nc.scalar.copy(out=spilled[h][:], in_=by_place(0)[:, vs, :])
-            nc.gpsimd.tensor_tensor(
-                out=shifted[0][:, vs, :],
-                in0=spilled[h][:],
-                in1=top[:, 0, vs].unsqueeze(2).to_broadcast([P, HV, D]),
-                op=ALU.subtract,
+        for h in range(2):
+            nc.vector.tensor_tensor(
+                out=total[:, h, :, :], in0=pair_sums[:, h, :, 0:HV], in1=pair_sums[:, h, :, HV : 2 * HV], op=ALU.add
             )
-        largest(1)
-        largest(2)
-        nc.scalar.activation(expd_first[0], shifted[0][:, halves[0], :], ACT.Exp)
-        shift(1, slice(0, V))
-        largest(3)
-        nc.scalar.activation(expd_first[1], shifted[0][:, halves[1], :], ACT.Exp)
-        shift(2, slice(0, V))
-        for vs in halves:
-            shift(PACK - 1, vs)
         for h, vs in enumerate(halves):
-            nc.vector.tensor_reduce(out=total[:, 0, vs], in_=expd_first[h], axis=AX.X, op=ALU.add)
-        for t in range(1, PACK):
-            nc.vector.tensor_reduce(out=total[:, t, :], in_=expd[t][:], axis=AX.X, op=ALU.add)
-        for vs in halves:
-            nc.scalar.activation(logs[:, :, vs], total[:, :, vs], ACT.Ln)
+            nc.scalar.activation(logs[:, :, vs], total[:, h, :, :], ACT.Ln)
         for vs in halves:
             nc.vector.tensor_tensor(out=result[:, :, vs], in0=logs[:, :, vs], in1=top[:, :, vs], op=ALU.add)
         nc.sync.dma_start(out=out_0.rearrange("(p t) v -> p t v", t=PACK), in_=result[:])

@@ -35,13 +35,14 @@ def tile_picked_lsep_none_lo_kernel(tc, xT, w1, offs, out_0, out_1, out_2):
 
         x_rows = xT.rearrange("(p j) t -> p j t", j=PACK)
         w_rows = w1.rearrange("(p j) m -> p j m", j=PACK)
-        HT = T // 2
+        x_cuts = [[0,512,1024],[0,512,1024]]
         x_raw = {}
         for a in range(2):
-            for h in range(2):
-                x_raw[a, h] = sb.tile([P, 2, HT], F32, name="x_raw%d%d" % (a, h))
-                nc.sync.dma_start(out=x_raw[a, h][:], in_=x_rows[:, 2 * a : 2 * a + 2, h * HT : (h + 1) * HT])
-                if (a, h) == (0, 0):
+            for c in range(len(x_cuts[a]) - 1):
+                lo, hi = x_cuts[a][c], x_cuts[a][c + 1]
+                x_raw[a, c] = sb.tile([P, 2, hi - lo], F32, name="x_raw%d%d" % (a, c))
+                nc.sync.dma_start(out=x_raw[a, c][:], in_=x_rows[:, 2 * a : 2 * a + 2, lo:hi])
+                if (a, c) == (0, 0):
                     nc.sync.dma_start(offsets[:], offs)
         w_cuts = [0, 128, 256, 384, 512]
         w_raw = []
@@ -52,32 +53,36 @@ def tile_picked_lsep_none_lo_kernel(tc, xT, w1, offs, out_0, out_1, out_2):
         pairs = [sb.tile([P, T], U32, name="pairs%d" % a, align_bytes=64) for a in range(2)]
         picked = sb.tile([P, 2, S], U32, name="picked", align_bytes=64)
 
-        def cast_x(copy, a, h, lo, hi):
-            copy(
-                out=pairs[a][:, h * HT + lo : h * HT + hi].bitcast(BF16).rearrange("p (c e) -> p c e", e=2),
-                in_=x_raw[a, h][:, :, lo:hi].rearrange("p e c -> p c e"),
-            )
+        def cast_x(a, c, on_scalar):
+            base, width = x_cuts[a][c], x_cuts[a][c + 1] - x_cuts[a][c]
+            for copy, lo, hi in ((nc.scalar.copy, 0, on_scalar), (nc.vector.tensor_copy, on_scalar, width)):
+                if hi > lo:
+                    copy(
+                        out=pairs[a][:, base + lo : base + hi].bitcast(BF16).rearrange("p (c e) -> p c e", e=2),
+                        in_=x_raw[a, c][:, :, lo:hi].rearrange("p e c -> p c e"),
+                    )
 
-        X_SCALAR = 160
-        cast_x(nc.vector.tensor_copy, 0, 0, 0, HT)
-        cast_x(nc.vector.tensor_copy, 0, 1, 0, HT)
-        nc.vector.tensor_copy(picked[:, 0, :], pairs[0][:].indirect(offsets[:]))
-        cast_x(nc.scalar.copy, 1, 0, 0, HT)
-        cast_x(nc.scalar.copy, 1, 1, 0, X_SCALAR)
-        cast_x(nc.vector.tensor_copy, 1, 1, X_SCALAR, HT)
         HS = S // 2
-        for h in range(2):
+        x_shares = [[0,0],[512,160]]
+        for c, share in enumerate(x_shares[0]):
+            cast_x(0, c, share)
+        nc.vector.tensor_copy(picked[:, 0, :], pairs[0][:].indirect(offsets[:]))
+        for c, share in enumerate(x_shares[1]):
+            cast_x(1, c, share)
+        for g in range(2):
             nc.vector.tensor_copy(
-                picked[:, 1, h * HS : (h + 1) * HS],
-                pairs[1][:].indirect(offsets[:, h * HS // 16 : (h + 1) * HS // 16]),
+                picked[:, 1, g * HS : (g + 1) * HS],
+                pairs[1][:].indirect(offsets[:, g * HS // 16 : (g + 1) * HS // 16]),
             )
 
         w_grouped = sb.tile([P, PACK, P, PACK], BF16, name="w_grouped", align_bytes=64)
         for c in range(len(w_raw)):
-            nc.scalar.copy(
-                out=w_grouped[:, :, w_cuts[c] // PACK : w_cuts[c + 1] // PACK, :].rearrange("p t m j -> p m j t"),
-                in_=w_raw[c][:].rearrange("p j (m t) -> p m j t", t=PACK),
-            )
+            last = c == len(w_raw) - 1
+            for ts in [slice(0, 2), slice(2, 4)] if last else [slice(0, 4)]:
+                nc.scalar.copy(
+                    out=w_grouped[:, ts, w_cuts[c] // PACK : w_cuts[c + 1] // PACK, :].rearrange("p t m j -> p m j t"),
+                    in_=w_raw[c][:].rearrange("p j (m t) -> p m j t", t=PACK)[:, :, :, ts],
+                )
 
         x_grouped = [sb.tile([P, HS * PACK], BF16, name="x_grouped%d" % h, align_bytes=64) for h in range(2)]
         x_codes = sb.tile([P, S], U32, name="x_codes", align_bytes=64)
@@ -147,27 +152,37 @@ def tile_picked_lsep_none_lo_kernel(tc, xT, w1, offs, out_0, out_1, out_2):
             nc.scalar.activation(expd[:, hs, t, :], shifted[t][:, hs, :], ACT.Exp)
 
         one = [slice(0, 1), slice(1, 2)]
-        largest(0, slice(0, V))
-        for h, hs in enumerate(one):
-            spilled = sb.tile([P, 1, D, HV], F32, name="spilled%d" % h)
-            nc.scalar.copy(out=spilled[:], in_=scores(0, hs))
-            shift(nc.gpsimd, spilled[:], 0, hs)
-        largest(1, slice(0, V))
-        largest(2, slice(0, V))
+
+        def spill(t, hs):
+            spilled = sb.tile([P, 1, D, HV], F32, name="spilled%d%d" % (t, hs.start))
+            nc.scalar.copy(out=spilled[:], in_=scores(t, hs))
+            shift(nc.gpsimd, spilled[:], t, hs)
+
+        def sub(t, hs):
+            shift(nc.vector, scores(t, hs), t, hs)
+
+        whole = slice(0, V)
+        largest(0, whole)
+        spill(0, one[0])
+        spill(0, one[1])
+        largest(1, whole)
+        largest(2, whole)
         exp(0, one[0])
-        for t in (1, 2):
-            shift(nc.vector, scores(t, both), t, both)
-            exp(t, both)
+        sub(1, both)
+        exp(1, both)
+        sub(2, both)
+        exp(2, both)
         exp(0, one[1])
-        for vs in halves:
-            largest(3, vs)
-        for hs in one:
-            shift(nc.vector, scores(3, hs), 3, hs)
-            exp(3, hs)
+        largest(3, halves[0])
+        largest(3, halves[1])
+        sub(3, one[0])
+        exp(3, one[0])
+        sub(3, one[1])
+        exp(3, one[1])
 
         pair_sums = sb.tile([P, 2, PACK, 2 * HV], F32, name="pair_sums")
         total = sb.tile([P, 2, PACK, HV], F32, name="total")
-        for hs, ts in ((both, slice(0, PACK - 1)), (one[0], slice(PACK - 1, PACK)), (one[1], slice(PACK - 1, PACK))):
+        for hs, ts in ((slice(0, 2), slice(0, PACK - 1)), (slice(0, 1), slice(PACK - 1, PACK)), (slice(1, 2), slice(PACK - 1, PACK))):
             nc.vector.tensor_tensor(
                 out=pair_sums[:, hs, ts, :], in0=expd[:, hs, ts, 0 : 2 * HV], in1=expd[:, hs, ts, 2 * HV : 4 * HV], op=ALU.add
             )
@@ -175,20 +190,29 @@ def tile_picked_lsep_none_lo_kernel(tc, xT, w1, offs, out_0, out_1, out_2):
             nc.vector.tensor_tensor(
                 out=total[:, h, :, :], in0=pair_sums[:, h, :, 0:HV], in1=pair_sums[:, h, :, HV : 2 * HV], op=ALU.add
             )
-        for h, vs in enumerate(halves):
-            nc.scalar.activation(logs[:, :, vs], total[:, h, :, :], ACT.Ln)
-        for vs in halves:
-            nc.vector.tensor_tensor(out=result[:, :, vs], in0=logs[:, :, vs], in1=top[:, :, vs], op=ALU.add)
-        nc.sync.dma_start(out=out_0.rearrange("(p t) v -> p t v", t=PACK), in_=result[:])
-
+        QV = HV // 2
+        quarters = [slice(q * QV, (q + 1) * QV) for q in range(4)]
         y_grouped = [sb.tile([P, HV * PACK], BF16, name="y_grouped%d" % h, align_bytes=64) for h in range(2)]
         y_codes = sb.tile([P, V], U32, name="y_codes", align_bytes=64)
         y_scales = sb.tile([P, V], U8, name="y_scales", align_bytes=64)
-        for h, vs in enumerate(halves):
-            nc.vector.tensor_copy(
-                out=y_grouped[h][:].rearrange("p (v t) -> p v t", t=PACK),
-                in_=result[:, :, vs].rearrange("p t v -> p v t"),
-            )
+
+        def by_lines(rows):
+            return rows.rearrange("p t (c i) -> p c t i", i=4)
+
+        def grouped(q):
+            part = y_grouped[q // 2][:, (q % 2) * QV * PACK : (q % 2 + 1) * QV * PACK]
+            return part.rearrange("p (c i t) -> p c t i", i=4, t=PACK)
+
+        for q, vs in enumerate(quarters):
+            nc.scalar.activation(logs[:, :, vs], total[:, q // 2, :, (q % 2) * QV : (q % 2 + 1) * QV], ACT.Ln)
+        for q, vs in enumerate(quarters):
+            nc.vector.tensor_tensor(out=result[:, :, vs], in0=logs[:, :, vs], in1=top[:, :, vs], op=ALU.add)
+        nc.sync.dma_start(out=out_0.rearrange("(p t) v -> p t v", t=PACK), in_=result[:])
+        for q in (0, 1):
+            nc.scalar.copy(out=grouped(q), in_=by_lines(result[:, :, quarters[q]]))
+        vs = quarters[3]
+        nc.vector.tensor_tensor(out=grouped(3), in0=by_lines(logs[:, :, vs]), in1=by_lines(top[:, :, vs]), op=ALU.add)
+        nc.vector.tensor_copy(out=grouped(2), in_=by_lines(result[:, :, quarters[2]]))
         for h, vs in enumerate(halves):
             nc.vector.quantize_mx(out=y_codes[:, vs].bitcast(FP8X4), scales=y_scales[:, vs], in_=y_grouped[h][:])
         nc.scalar.dma_start(

@@ -35,14 +35,15 @@ def tile_picked_lsep_none_lo_kernel(tc, xT, w1, offs, out_0, out_1, out_2):
 
         x_rows = xT.rearrange("(p j) t -> p j t", j=PACK)
         w_rows = w1.rearrange("(p j) m -> p j m", j=PACK)
-        x_cuts = [[0,512,1024],[0,512,1024]]
+        x_cuts = [[0,256,768,1024],[0,512,1024]]
         x_raw = {}
         for a in range(2):
             for c in range(len(x_cuts[a]) - 1):
                 lo, hi = x_cuts[a][c], x_cuts[a][c + 1]
                 x_raw[a, c] = sb.tile([P, 2, hi - lo], F32, name="x_raw%d%d" % (a, c))
-                nc.sync.dma_start(out=x_raw[a, c][:], in_=x_rows[:, 2 * a : 2 * a + 2, lo:hi])
-                if (a, c) == (0, 0):
+                queue = nc.scalar if (a, c) == (0, 0) else nc.sync
+                queue.dma_start(out=x_raw[a, c][:], in_=x_rows[:, 2 * a : 2 * a + 2, lo:hi])
+                if (a, c) == (0, 1):
                     nc.sync.dma_start(offsets[:], offs)
         w_cuts = [0, 128, 256, 384, 512]
         w_raw = []
@@ -63,7 +64,7 @@ def tile_picked_lsep_none_lo_kernel(tc, xT, w1, offs, out_0, out_1, out_2):
                     )
 
         HS = S // 2
-        x_shares = [[0,0],[512,160]]
+        x_shares = [[256,0,80],[512,160]]
         for c, share in enumerate(x_shares[0]):
             cast_x(0, c, share)
         nc.vector.tensor_copy(picked[:, 0, :], pairs[0][:].indirect(offsets[:]))
@@ -220,5 +221,5 @@ def tile_picked_lsep_none_lo_kernel(tc, xT, w1, offs, out_0, out_1, out_2):
         )
         scale_rows = out_2.rearrange("z q c -> (z q) c").bitcast(I32)
         for q in range(4):
-            eng = nc.sync if q % 2 == 0 else nc.scalar
+            eng = nc.scalar if q == 1 else nc.sync
             eng.dma_start(out=scale_rows[4 * q : 4 * q + 4, :], in_=y_scales[32 * q : 32 * q + 4, :].bitcast(I32))

@@ -35,46 +35,37 @@ def tile_picked_lsep_none_lo_kernel(tc, xT, w1, offs, out_0, out_1, out_2):
 
         x_rows = xT.rearrange("(p j) t -> p j t", j=PACK)
         w_rows = w1.rearrange("(p j) m -> p j m", j=PACK)
-        x_cuts = [[0,256,768,1024],[0,512,1024]]
-        x_raw = {}
-        for a in range(2):
-            for c in range(len(x_cuts[a]) - 1):
-                lo, hi = x_cuts[a][c], x_cuts[a][c + 1]
-                x_raw[a, c] = sb.tile([P, 2, hi - lo], F32, name="x_raw%d%d" % (a, c))
-                queue = nc.scalar if (a, c) == (0, 0) else nc.sync
-                queue.dma_start(out=x_raw[a, c][:], in_=x_rows[:, 2 * a : 2 * a + 2, lo:hi])
-                if (a, c) == (0, 1):
-                    nc.sync.dma_start(offsets[:], offs)
+        planes = [sb.tile([P, T], F32, name="plane%d" % j) for j in range(PACK)]
+        nc.scalar.dma_start(out=planes[0][:, : T // 2], in_=x_rows[:, 0, : T // 2])
+        nc.sync.dma_start(out=planes[0][:, T // 2 :], in_=x_rows[:, 0, T // 2 :])
+        nc.sync.dma_start(offsets[:], offs)
+        for j in range(1, PACK):
+            nc.sync.dma_start(out=planes[j][:], in_=x_rows[:, j, :])
         w_cuts = [0, 128, 256, 384, 512]
         w_raw = []
         for c in range(len(w_cuts) - 1):
             w_raw.append(sb.tile([P, PACK, w_cuts[c + 1] - w_cuts[c]], F32, name="w_raw%d" % c))
             nc.sync.dma_start(out=w_raw[c][:], in_=w_rows[:, :, w_cuts[c] : w_cuts[c + 1]])
 
-        pairs = [sb.tile([P, T], U32, name="pairs%d" % a, align_bytes=64) for a in range(2)]
-        picked = sb.tile([P, 2, S], U32, name="picked", align_bytes=64)
-
-        def cast_x(a, c, on_scalar):
-            base, width = x_cuts[a][c], x_cuts[a][c + 1] - x_cuts[a][c]
-            for copy, lo, hi in ((nc.scalar.copy, 0, on_scalar), (nc.vector.tensor_copy, on_scalar, width)):
-                if hi > lo:
-                    copy(
-                        out=pairs[a][:, base + lo : base + hi].bitcast(BF16).rearrange("p (c e) -> p c e", e=2),
-                        in_=x_raw[a, c][:, :, lo:hi].rearrange("p e c -> p c e"),
-                    )
-
         HS = S // 2
-        x_shares = [[256,0,80],[512,160]]
-        for c, share in enumerate(x_shares[0]):
-            cast_x(0, c, share)
-        nc.vector.tensor_copy(picked[:, 0, :], pairs[0][:].indirect(offsets[:]))
-        for c, share in enumerate(x_shares[1]):
-            cast_x(1, c, share)
-        for g in range(2):
-            nc.vector.tensor_copy(
-                picked[:, 1, g * HS : (g + 1) * HS],
-                pairs[1][:].indirect(offsets[:, g * HS // 16 : (g + 1) * HS // 16]),
+        picked = [sb.tile([P, 2, S], F32, name="picked%d" % a) for a in range(2)]
+        x_grouped = [sb.tile([P, HS * PACK], BF16, name="x_grouped%d" % h, align_bytes=64) for h in range(2)]
+
+        def round_pair(copy, a, h):
+            copy(
+                out=x_grouped[h][:].rearrange("p (n j) -> p n j", j=PACK)[:, :, 2 * a : 2 * a + 2],
+                in_=picked[a][:, :, h * HS : (h + 1) * HS].rearrange("p e n -> p n e"),
             )
+
+        for a in range(2):
+            nc.vector.tensor_copy(picked[a][:, 0, :], planes[2 * a][:].indirect(offsets[:]))
+            for h in range(2):
+                nc.vector.tensor_copy(
+                    picked[a][:, 1, h * HS : (h + 1) * HS],
+                    planes[2 * a + 1][:].indirect(offsets[:, h * HS // 16 : (h + 1) * HS // 16]),
+                )
+        for h in range(2):
+            round_pair(nc.scalar.copy, 0, h)
 
         w_grouped = sb.tile([P, PACK, P, PACK], BF16, name="w_grouped", align_bytes=64)
         for c in range(len(w_raw)):
@@ -85,14 +76,10 @@ def tile_picked_lsep_none_lo_kernel(tc, xT, w1, offs, out_0, out_1, out_2):
                     in_=w_raw[c][:].rearrange("p j (m t) -> p m j t", t=PACK)[:, :, :, ts],
                 )
 
-        x_grouped = [sb.tile([P, HS * PACK], BF16, name="x_grouped%d" % h, align_bytes=64) for h in range(2)]
         x_codes = sb.tile([P, S], U32, name="x_codes", align_bytes=64)
         x_scales = sb.tile([P, S], U8, name="x_scales", align_bytes=64)
         for h in range(2):
-            nc.vector.tensor_copy(
-                out=x_grouped[h][:].bitcast(I32).rearrange("p (n a) -> p n a", a=2),
-                in_=picked[:, :, h * HS : (h + 1) * HS].bitcast(I32).rearrange("p a n -> p n a"),
-            )
+            round_pair(nc.vector.tensor_copy, 1, h)
         for h in range(2):
             nc.vector.quantize_mx(
                 out=x_codes[:, h * HS : (h + 1) * HS].bitcast(FP8X4),

@@ -41,11 +41,12 @@ def tile_picked_lsep_none_lo_kernel(tc, xT, w1, offs, out_0, out_1, out_2):
         nc.sync.dma_start(offsets[:], offs)
         for j in range(1, PACK):
             nc.sync.dma_start(out=planes[j][:], in_=x_rows[:, j, :])
-        w_cuts = [0, 128, 256, 384, 512]
-        w_raw = []
-        for c in range(len(w_cuts) - 1):
-            w_raw.append(sb.tile([P, PACK, w_cuts[c + 1] - w_cuts[c]], F32, name="w_raw%d" % c))
-            nc.sync.dma_start(out=w_raw[c][:], in_=w_rows[:, :, w_cuts[c] : w_cuts[c + 1]])
+        WC = N // 4
+        w_raw = [sb.tile([P, PACK, 2 * WC], F32, name="w_raw%d" % g) for g in range(2)]
+        for c in range(4):
+            nc.sync.dma_start(
+                out=w_raw[c // 2][:, :, (c % 2) * WC : (c % 2 + 1) * WC], in_=w_rows[:, :, c * WC : (c + 1) * WC]
+            )
 
         HS = S // 2
         picked = [sb.tile([P, 2, S], F32, name="picked%d" % a) for a in range(2)]
@@ -68,13 +69,20 @@ def tile_picked_lsep_none_lo_kernel(tc, xT, w1, offs, out_0, out_1, out_2):
             round_pair(nc.scalar.copy, 0, h)
 
         w_grouped = sb.tile([P, PACK, P, PACK], BF16, name="w_grouped", align_bytes=64)
-        for c in range(len(w_raw)):
-            last = c == len(w_raw) - 1
-            for ts in [slice(0, 2), slice(2, 4)] if last else [slice(0, 4)]:
-                nc.scalar.copy(
-                    out=w_grouped[:, ts, w_cuts[c] // PACK : w_cuts[c + 1] // PACK, :].rearrange("p t m j -> p m j t"),
-                    in_=w_raw[c][:].rearrange("p j (m t) -> p m j t", t=PACK)[:, :, :, ts],
-                )
+
+        def deal(lo, hi, ts):
+            g = lo // (2 * WC)
+            nc.scalar.copy(
+                out=w_grouped[:, ts, lo // PACK : hi // PACK, :].rearrange("p t m j -> p m j t"),
+                in_=w_raw[g][:, :, lo - 2 * WC * g : hi - 2 * WC * g].rearrange("p j (m t) -> p m j t", t=PACK)[:, :, :, ts],
+            )
+
+        deal(0, WC, slice(0, 4))
+        deal(WC, 2 * WC, slice(0, 4))
+        deal(2 * WC, 3 * WC, slice(0, 2))
+        deal(3 * WC, 4 * WC, slice(0, 1))
+        deal(3 * WC, 4 * WC, slice(1, 2))
+        deal(2 * WC, 4 * WC, slice(2, 4))
 
         x_codes = sb.tile([P, S], U32, name="x_codes", align_bytes=64)
         x_scales = sb.tile([P, S], U8, name="x_scales", align_bytes=64)

@@ -1,6 +1,7 @@
 from contextlib import ExitStack
 
 import concourse.mybir as mybir
+from concourse.masks import make_identity
 
 K, T, S, V, N = 512, 1024, 512, 128, 512
 D = S // V
@@ -41,151 +42,180 @@ def tile_picked_lsep_none_lo_kernel(tc, xT, w1, offs, out_0, out_1, out_2):
         nc.sync.dma_start(offsets[:], offs)
         for j in range(1, PACK):
             nc.sync.dma_start(out=planes[j][:], in_=x_rows[:, j, :])
-        WC = N // 4
-        w_raw = [sb.tile([P, PACK, 2 * WC], F32, name="w_raw%d" % g) for g in range(2)]
-        for c in range(4):
-            nc.sync.dma_start(
-                out=w_raw[c // 2][:, :, (c % 2) * WC : (c % 2 + 1) * WC], in_=w_rows[:, :, c * WC : (c + 1) * WC]
-            )
+        C = N // P
+        L = P // PACK
+        w_raw = [sb.tile([P, PACK, P], F32, name="w_raw%d" % c) for c in range(C)]
+        for c in range(C):
+            nc.sync.dma_start(out=w_raw[c][:], in_=w_rows[:, :, c * P : (c + 1) * P])
+        ident = sb.tile([P, P], F32, name="ident")
+        make_identity(nc, ident[:])
 
         HS = S // 2
-        picked = [sb.tile([P, 2, S], F32, name="picked%d" % a) for a in range(2)]
         x_grouped = [sb.tile([P, HS * PACK], BF16, name="x_grouped%d" % h, align_bytes=64) for h in range(2)]
+        picked = [sb.tile([P, 2, HS], BF16, name="picked%d" % a) for a in range(2)]
+        slots = [g[:].rearrange("p (n j) -> p n j", j=PACK) for g in x_grouped]
+        for j in range(PACK):
+            nc.scalar.activation(picked[j // 2][:, j % 2, :], planes[j][:].indirect(offsets[:, HS // 16 :]), ACT.Copy)
+            nc.vector.tensor_copy(slots[0][:, :, j], planes[j][:].indirect(offsets[:, : HS // 16]))
+            if j % 2:
+                nc.vector.tensor_copy(slots[1][:, :, j - 1 : j + 1], picked[j // 2][:].rearrange("p e n -> p n e"))
 
-        def round_pair(copy, a, h):
-            copy(
-                out=x_grouped[h][:].rearrange("p (n j) -> p n j", j=PACK)[:, :, 2 * a : 2 * a + 2],
-                in_=picked[a][:, :, h * HS : (h + 1) * HS].rearrange("p e n -> p n e"),
-            )
-
-        for a in range(2):
-            nc.vector.tensor_copy(picked[a][:, 0, :], planes[2 * a][:].indirect(offsets[:]))
-            for h in range(2):
-                nc.vector.tensor_copy(
-                    picked[a][:, 1, h * HS : (h + 1) * HS],
-                    planes[2 * a + 1][:].indirect(offsets[:, h * HS // 16 : (h + 1) * HS // 16]),
-                )
-        for h in range(2):
-            round_pair(nc.scalar.copy, 0, h)
-
-        w_grouped = sb.tile([P, PACK, P, PACK], BF16, name="w_grouped", align_bytes=64)
-
-        def deal(lo, hi, ts):
-            g = lo // (2 * WC)
+        w_grouped = [
+            sb.tile([P, PACK, L, PACK], BF16, name="w_grouped%d" % c, tag="slot%d" % c, align_bytes=64) for c in range(C)
+        ]
+        for c in range(C):
             nc.scalar.copy(
-                out=w_grouped[:, ts, lo // PACK : hi // PACK, :].rearrange("p t m j -> p m j t"),
-                in_=w_raw[g][:, :, lo - 2 * WC * g : hi - 2 * WC * g].rearrange("p j (m t) -> p m j t", t=PACK)[:, :, :, ts],
+                out=w_grouped[c][:].rearrange("p t l j -> p l j t"),
+                in_=w_raw[c][:].rearrange("p j (l t) -> p l j t", t=PACK),
             )
 
-        deal(0, WC, slice(0, 4))
-        deal(WC, 2 * WC, slice(0, 4))
-        deal(2 * WC, 3 * WC, slice(0, 2))
-        deal(3 * WC, 4 * WC, slice(0, 1))
-        deal(3 * WC, 4 * WC, slice(1, 2))
-        deal(2 * WC, 4 * WC, slice(2, 4))
-
-        x_codes = sb.tile([P, S], U32, name="x_codes", align_bytes=64)
+        x_codes = {0: sb.tile([P, HS], U32, name="x_codes0", align_bytes=64)}
         x_scales = sb.tile([P, S], U8, name="x_scales", align_bytes=64)
-        for h in range(2):
-            round_pair(nc.vector.tensor_copy, 1, h)
-        for h in range(2):
+        w_codes = [sb.tile([P, P], U32, name="w_codes%d" % c, align_bytes=64) for c in range(C - 1)]
+        w_codes.append(w_codes[0])
+        w_scales = [sb.tile([P, P], U8, name="w_scales%d" % c, align_bytes=64) for c in range(C)]
+        banks = [psum.tile([P, S], F32, name="bank%d" % c) for c in range(C)]
+
+        def quantise_x(h):
             nc.vector.quantize_mx(
-                out=x_codes[:, h * HS : (h + 1) * HS].bitcast(FP8X4),
+                out=x_codes[h][:].bitcast(FP8X4),
                 scales=x_scales[:, h * HS : (h + 1) * HS],
                 in_=x_grouped[h][:],
             )
 
-        w_codes = [sb.tile([P, P], U32, name="w_codes%d" % t, align_bytes=64) for t in range(PACK)]
-        w_scales = [sb.tile([P, P], U8, name="w_scales%d" % t, align_bytes=64) for t in range(PACK)]
-        banks = [psum.tile([P, S], F32, name="bank%d" % t) for t in range(PACK)]
-        for t in range(PACK):
+        def quantise_w(c):
             nc.vector.quantize_mx(
-                out=w_codes[t][:].bitcast(FP8X4),
-                scales=w_scales[t][:],
-                in_=w_grouped[:, t, :, :].rearrange("p m j -> p (m j)"),
+                out=w_codes[c][:].bitcast(FP8X4),
+                scales=w_scales[c][:],
+                in_=w_grouped[c][:].rearrange("p t l j -> p (t l j)"),
             )
-            nc.tensor.matmul_mx(
-                out=banks[t][:],
-                lhsT=w_codes[t][:].bitcast(FP8X4),
-                lhsT_scale=w_scales[t][:],
-                rhs=x_codes[:].bitcast(FP8X4),
-                rhs_scale=x_scales[:],
-                start=True,
-                stop=True,
-            )
+
+        def products(c):
+            for d in range(D):
+                nc.tensor.matmul_mx(
+                    out=banks[c][:, d * V : (d + 1) * V],
+                    lhsT=x_codes[d // 2][:, (d % 2) * V : (d % 2 + 1) * V].bitcast(FP8X4),
+                    lhsT_scale=x_scales[:, d * V : (d + 1) * V],
+                    rhs=w_codes[c][:].bitcast(FP8X4),
+                    rhs_scale=w_scales[c][:],
+                    start=True,
+                    stop=True,
+                )
+
+        quantise_x(0)
+        quantise_w(0)
+        x_codes[1] = sb.tile([P, HS], U32, name="x_codes1", tag="slot0", align_bytes=64)
+        quantise_x(1)
+        products(0)
+        for c in range(1, C - 1):
+            quantise_w(c)
+            products(c)
 
         HV = V // 2
         halves = [slice(0, HV), slice(HV, V)]
         both = slice(0, 2)
-        top = sb.tile([P, PACK, V], F32, name="top")
+        tops = sb.tile([P, 2, 2, C, L], F32, name="tops", tag="slot2", align_bytes=64)
         logs = sb.tile([P, PACK, V], F32, name="logs")
         result = sb.tile([P, PACK, V], F32, name="result")
-        expd = sb.tile([P, 2, PACK + 1, D * HV], F32, name="expd")
-        shifted = {t: sb.tile([P, 2, D * HV], F32, name="shifted%d" % t)[:] for t in (0, 2, 3)}
-        shifted[1] = expd[:].rearrange("p h s n -> p (h s) n")[:, PACK : PACK + 2, :]
+        expd = sb.tile([P, 2, C + 1, D * HV], F32, name="expd")
+        shifted = {c: sb.tile([P, 2, D * HV], F32, name="shifted%d" % c)[:] for c in (0, 2, 3)}
+        shifted[1] = expd[:].rearrange("p h s n -> p (h s) n")[:, C : C + 2, :]
 
-        def scores(t, hs):
-            return banks[t][:].rearrange("p (d h v) -> p h d v", d=D, h=2)[:, hs, :, :]
-
-        def largest(t, vs):
+        def largest(c, hs):
             nc.vector.tensor_reduce(
-                out=top[:, t, vs],
-                in_=banks[t][:].rearrange("p (d v) -> p v d", d=D)[:, vs, :],
+                out=tops[:, hs, :, c, :].rearrange("p h u l -> p (h u) l"),
+                in_=banks[c][:].rearrange("p (d t l) -> p t l d", d=D, l=L)[:, 2 * hs.start : 2 * hs.stop, :, :],
                 axis=AX.X,
                 op=ALU.max,
             )
 
-        def shift(eng, src, t, hs):
-            tops = top[:, t, :].rearrange("p (h v) -> p h v", h=2)[:, hs, :]
+        def scores(c, h):
+            return banks[c][:].rearrange("p (d h u l) -> p h d u l", d=D, h=2, u=2)[:, h, :, :, :]
+
+        def shift(eng, src, c, h):
             eng.tensor_tensor(
-                out=shifted[t][:, hs, :].rearrange("p h (d v) -> p h d v", d=D),
+                out=shifted[c][:, h, :].rearrange("p (d u l) -> p d u l", d=D, u=2),
                 in0=src,
-                in1=tops.unsqueeze(2).to_broadcast([P, hs.stop - hs.start, D, HV]),
+                in1=tops[:, h, :, c, :].unsqueeze(1).to_broadcast([P, D, 2, L]),
                 op=ALU.subtract,
             )
 
-        def exp(t, hs):
-            nc.scalar.activation(expd[:, hs, t, :], shifted[t][:, hs, :], ACT.Exp)
+        def exp(c, hs):
+            nc.scalar.activation(expd[:, hs, c, :], shifted[c][:, hs, :], ACT.Exp)
 
         one = [slice(0, 1), slice(1, 2)]
 
-        def spill(t, hs):
-            spilled = sb.tile([P, 1, D, HV], F32, name="spilled%d%d" % (t, hs.start))
-            nc.scalar.copy(out=spilled[:], in_=scores(t, hs))
-            shift(nc.gpsimd, spilled[:], t, hs)
+        def spill(c, h):
+            spilled = sb.tile([P, D, 2, L], F32, name="spilled%d%d" % (c, h))
+            nc.scalar.copy(out=spilled[:], in_=scores(c, h))
+            shift(nc.gpsimd, spilled[:], c, h)
 
-        def sub(t, hs):
-            shift(nc.vector, scores(t, hs), t, hs)
+        def sub_whole(c):
+            nc.vector.tensor_tensor(
+                out=shifted[c].rearrange("p h (t l) -> p (h t) l", l=L).rearrange("p (d t) l -> p d t l", d=D),
+                in0=banks[c][:].rearrange("p (d t l) -> p d t l", d=D, l=L),
+                in1=tops[:, :, :, c, :].rearrange("p h u l -> p (h u) l").unsqueeze(1).to_broadcast([P, D, PACK, L]),
+                op=ALU.subtract,
+            )
 
-        whole = slice(0, V)
-        largest(0, whole)
-        spill(0, one[0])
-        spill(0, one[1])
-        largest(1, whole)
-        largest(2, whole)
+        def exp_whole(c):
+            nc.scalar.activation(
+                expd[:, :, c, :].rearrange("p h (d n) -> p d h n", d=D),
+                shifted[c].rearrange("p h n -> p (h n)").rearrange("p (d h n) -> p d h n", d=D, h=2),
+                ACT.Exp,
+            )
+
+        largest(0, both)
+        spill(0, 0)
+        spill(0, 1)
+        largest(1, both)
+        quantise_w(3)
+        products(3)
         exp(0, one[0])
-        sub(1, both)
-        exp(1, both)
-        sub(2, both)
-        exp(2, both)
+        sub_whole(1)
+        exp_whole(1)
+        largest(2, both)
         exp(0, one[1])
-        largest(3, halves[0])
-        largest(3, halves[1])
-        sub(3, one[0])
+        sub_whole(2)
+        exp_whole(2)
+        largest(3, one[0])
+        largest(3, one[1])
+        shift(nc.vector, scores(3, 0), 3, 0)
         exp(3, one[0])
-        sub(3, one[1])
+        shift(nc.vector, scores(3, 1), 3, 1)
         exp(3, one[1])
 
-        pair_sums = sb.tile([P, 2, PACK, 2 * HV], F32, name="pair_sums")
-        total = sb.tile([P, 2, PACK, HV], F32, name="total")
-        for hs, ts in ((slice(0, 2), slice(0, PACK - 1)), (slice(0, 1), slice(PACK - 1, PACK)), (slice(1, 2), slice(PACK - 1, PACK))):
-            nc.vector.tensor_tensor(
-                out=pair_sums[:, hs, ts, :], in0=expd[:, hs, ts, 0 : 2 * HV], in1=expd[:, hs, ts, 2 * HV : 4 * HV], op=ALU.add
+        top_bank = psum.tile([P, PACK, V], F32, name="top_bank")
+        sum_bank = psum.tile([P, PACK, V], F32, name="sum_bank")
+        for t in range(PACK):
+            nc.tensor.transpose(top_bank[:, t, :], tops[:, t // 2, t % 2, :, :].rearrange("p c l -> p (c l)"), ident[:])
+
+        pair_sums = sb.tile([P, 2, C, 2 * HV], F32, name="pair_sums")
+        sums = sb.tile([P, 2, 2, C, L], F32, name="sums")
+
+        def add_pairs(eng, hs, cs):
+            eng.tensor_tensor(
+                out=pair_sums[:, hs, cs, :], in0=expd[:, hs, cs, 0 : 2 * HV], in1=expd[:, hs, cs, 2 * HV : 4 * HV], op=ALU.add
             )
-        for h in range(2):
+
+        def add_up(h):
             nc.vector.tensor_tensor(
-                out=total[:, h, :, :], in0=pair_sums[:, h, :, 0:HV], in1=pair_sums[:, h, :, HV : 2 * HV], op=ALU.add
+                out=sums[:, h, :, :, :].rearrange("p u c l -> p c u l"),
+                in0=pair_sums[:, h, :, 0:HV].rearrange("p c (u l) -> p c u l", u=2),
+                in1=pair_sums[:, h, :, HV : 2 * HV].rearrange("p c (u l) -> p c u l", u=2),
+                op=ALU.add,
             )
+            for u in range(2):
+                nc.tensor.transpose(sum_bank[:, 2 * h + u, :], sums[:, h, u, :, :].rearrange("p c l -> p (c l)"), ident[:])
+
+        add_pairs(nc.gpsimd, both, slice(1, 2))
+        add_pairs(nc.gpsimd, both, slice(0, 1))
+        add_pairs(nc.vector, one[0], slice(2, 4))
+        add_pairs(nc.vector, one[1], slice(2, 3))
+        add_up(0)
+        add_pairs(nc.vector, one[1], slice(3, 4))
+        add_up(1)
+        top = top_bank
         QV = HV // 2
         quarters = [slice(q * QV, (q + 1) * QV) for q in range(4)]
         y_grouped = [sb.tile([P, HV * PACK], BF16, name="y_grouped%d" % h, align_bytes=64) for h in range(2)]
@@ -200,7 +230,7 @@ def tile_picked_lsep_none_lo_kernel(tc, xT, w1, offs, out_0, out_1, out_2):
             return part.rearrange("p (c i t) -> p c t i", i=4, t=PACK)
 
         for q, vs in enumerate(quarters):
-            nc.scalar.activation(logs[:, :, vs], total[:, q // 2, :, (q % 2) * QV : (q % 2 + 1) * QV], ACT.Ln)
+            nc.scalar.activation(logs[:, :, vs], sum_bank[:, :, vs], ACT.Ln)
         for q, vs in enumerate(quarters):
             nc.vector.tensor_tensor(out=result[:, :, vs], in0=logs[:, :, vs], in1=top[:, :, vs], op=ALU.add)
         nc.sync.dma_start(out=out_0.rearrange("(p t) v -> p t v", t=PACK), in_=result[:])

@@ -190,31 +190,40 @@ def tile_picked_lsep_none_lo_kernel(tc, xT, w1, offs, out_0, out_1, out_2):
         for t in range(PACK):
             nc.tensor.transpose(top_bank[:, t, :], tops[:, t // 2, t % 2, :, :].rearrange("p c l -> p (c l)"), ident[:])
 
-        pair_sums = sb.tile([P, 2, C, 2 * HV], F32, name="pair_sums")
-        sums = sb.tile([P, 2, 2, C, L], F32, name="sums")
+        pair_sums = sb.tile([P, 2, 2, 2, C, L], F32, name="pair_sums")
+        sums = sb.tile([P, 2, P], F32, name="sums")
 
-        def add_pairs(eng, hs, cs):
-            eng.tensor_tensor(
-                out=pair_sums[:, hs, cs, :], in0=expd[:, hs, cs, 0 : 2 * HV], in1=expd[:, hs, cs, 2 * HV : 4 * HV], op=ALU.add
-            )
-
-        def add_up(h):
+        def add_pairs(h, cs):
+            terms = expd[:, h, cs, :].rearrange("p c (e q l) -> p e c q l", e=2, l=L)
             nc.vector.tensor_tensor(
-                out=sums[:, h, :, :, :].rearrange("p u c l -> p c u l"),
-                in0=pair_sums[:, h, :, 0:HV].rearrange("p c (u l) -> p c u l", u=2),
-                in1=pair_sums[:, h, :, HV : 2 * HV].rearrange("p c (u l) -> p c u l", u=2),
+                out=pair_sums[:, h, :, :, cs, :].rearrange("p s u c l -> p c (s u) l"),
+                in0=terms[:, 0, :, :, :],
+                in1=terms[:, 1, :, :, :],
                 op=ALU.add,
             )
-            for u in range(2):
-                nc.tensor.transpose(sum_bank[:, 2 * h + u, :], sums[:, h, u, :, :].rearrange("p c l -> p (c l)"), ident[:])
 
-        add_pairs(nc.gpsimd, both, slice(1, 2))
-        add_pairs(nc.gpsimd, both, slice(0, 1))
-        add_pairs(nc.vector, one[0], slice(2, 4))
-        add_pairs(nc.vector, one[1], slice(2, 3))
-        add_up(0)
-        add_pairs(nc.vector, one[1], slice(3, 4))
-        add_up(1)
+        add_pairs(0, slice(0, 3))
+        add_pairs(0, slice(3, 4))
+        add_pairs(1, slice(1, 3))
+        add_pairs(1, slice(0, 4, 3))
+        for u in range(2):
+            for s in range(2):
+                nc.tensor.matmul(
+                    sum_bank[:, u, :],
+                    lhsT=pair_sums[:, 0, s, u, :, :].rearrange("p c l -> p (c l)"),
+                    rhs=ident[:],
+                    is_transpose=True,
+                    start=(s == 0),
+                    stop=(s == 1),
+                )
+        nc.vector.tensor_tensor(
+            out=sums[:].rearrange("p u n -> p (u n)"),
+            in0=pair_sums[:, 1, 0, :, :, :].rearrange("p u c l -> p (u c l)"),
+            in1=pair_sums[:, 1, 1, :, :, :].rearrange("p u c l -> p (u c l)"),
+            op=ALU.add,
+        )
+        for u in range(2):
+            nc.tensor.transpose(sum_bank[:, 2 + u, :], sums[:, u, :], ident[:])
         top = top_bank
         QV = HV // 2
         quarters = [slice(q * QV, (q + 1) * QV) for q in range(4)]

@@ -76,11 +76,11 @@ def tile_picked_lsep_none_lo_kernel(tc, xT, w1, offs, out_0, out_1, out_2):
         w_scales = [sb.tile([P, P], U8, name="w_scales%d" % c, align_bytes=64) for c in range(C)]
         banks = [psum.tile([P, S], F32, name="bank%d" % c) for c in range(C)]
 
-        def quantise_x(h):
+        def quantise_x(h, lo, hi):
             nc.vector.quantize_mx(
-                out=x_codes[h][:].bitcast(FP8X4),
-                scales=x_scales[:, h * HS : (h + 1) * HS],
-                in_=x_grouped[h][:],
+                out=x_codes[h][:, lo:hi].bitcast(FP8X4),
+                scales=x_scales[:, h * HS + lo : h * HS + hi],
+                in_=x_grouped[h][:, lo * PACK : hi * PACK],
             )
 
         def quantise_w(c):
@@ -102,10 +102,11 @@ def tile_picked_lsep_none_lo_kernel(tc, xT, w1, offs, out_0, out_1, out_2):
                     stop=True,
                 )
 
-        quantise_x(0)
+        quantise_x(0, 0, HS)
         quantise_w(0)
         x_codes[1] = sb.tile([P, HS], U32, name="x_codes1", tag="slot0", align_bytes=64)
-        quantise_x(1)
+        quantise_x(1, 0, V)
+        quantise_x(1, V, HS)
         products(0)
         for c in range(1, C - 1):
             quantise_w(c)
@@ -216,13 +217,13 @@ def tile_picked_lsep_none_lo_kernel(tc, xT, w1, offs, out_0, out_1, out_2):
                     start=(s == 0),
                     stop=(s == 1),
                 )
-        nc.vector.tensor_tensor(
-            out=sums[:].rearrange("p u n -> p (u n)"),
-            in0=pair_sums[:, 1, 0, :, :, :].rearrange("p u c l -> p (u c l)"),
-            in1=pair_sums[:, 1, 1, :, :, :].rearrange("p u c l -> p (u c l)"),
-            op=ALU.add,
-        )
         for u in range(2):
+            nc.vector.tensor_tensor(
+                out=sums[:, u, :],
+                in0=pair_sums[:, 1, 0, u, :, :].rearrange("p c l -> p (c l)"),
+                in1=pair_sums[:, 1, 1, u, :, :].rearrange("p c l -> p (c l)"),
+                op=ALU.add,
+            )
             nc.tensor.transpose(sum_bank[:, 2 + u, :], sums[:, u, :], ident[:])
         top = top_bank
         QV = HV // 2

@@ -119,7 +119,7 @@ def tile_picked_lsep_none_lo_kernel(tc, xT, w1, offs, out_0, out_1, out_2):
         logs = sb.tile([P, PACK, V], F32, name="logs")
         result = sb.tile([P, PACK, V], F32, name="result")
         expd = sb.tile([P, 2, C + 1, D * HV], F32, name="expd")
-        shifted = {c: sb.tile([P, 2, D * HV], F32, name="shifted%d" % c)[:] for c in (0, 2, 3)}
+        shifted = {c: sb.tile([P, 2, D * HV], F32, name="shifted%d" % c)[:] for c in (2, 3)}
         shifted[1] = expd[:].rearrange("p h s n -> p (h s) n")[:, C : C + 2, :]
 
         def largest(c, hs):
@@ -167,11 +167,12 @@ def tile_picked_lsep_none_lo_kernel(tc, xT, w1, offs, out_0, out_1, out_2):
             )
 
         largest(0, both)
+        quantise_w(3)
+        products(3)
+        shifted[0] = sb.tile([P, 2, D * HV], F32, name="shifted0", tag="slot3", align_bytes=64)[:]
         spill(0, 0)
         spill(0, 1)
         largest(1, both)
-        quantise_w(3)
-        products(3)
         exp(0, one[0])
         sub_whole(1)
         exp_whole(1)

@@ -37,9 +37,10 @@ def tile_picked_lsep_none_lo_kernel(tc, xT, w1, offs, out_0, out_1, out_2):
         x_rows = xT.rearrange("(p j) t -> p j t", j=PACK)
         w_rows = w1.rearrange("(p j) m -> p j m", j=PACK)
         planes = [sb.tile([P, T], F32, name="plane%d" % j) for j in range(PACK)]
-        nc.scalar.dma_start(out=planes[0][:, : T // 2], in_=x_rows[:, 0, : T // 2])
-        nc.sync.dma_start(out=planes[0][:, T // 2 :], in_=x_rows[:, 0, T // 2 :])
+        CUT = 5 * T // 8
+        nc.scalar.dma_start(out=planes[0][:, :CUT], in_=x_rows[:, 0, :CUT])
         nc.sync.dma_start(offsets[:], offs)
+        nc.sync.dma_start(out=planes[0][:, CUT:], in_=x_rows[:, 0, CUT:])
         for j in range(1, PACK):
             nc.sync.dma_start(out=planes[j][:], in_=x_rows[:, j, :])
         C = N // P

@@ -196,19 +196,30 @@ def tile_picked_lsep_none_lo_kernel(tc, xT, w1, offs, out_0, out_1, out_2):
         pair_sums = sb.tile([P, 2, 2, 2, C, L], F32, name="pair_sums")
         sums = sb.tile([P, 2, P], F32, name="sums")
 
-        def add_pairs(h, cs):
+        def add_chunk(eng, c):
+            terms = expd[:, :, c, :].rearrange("p h (e q l) -> p e h q l", e=2, l=L)
+            eng.tensor_tensor(
+                out=pair_sums[:, :, :, :, c, :].rearrange("p h s u l -> p h (s u) l"),
+                in0=terms[:, 0, :, :, :],
+                in1=terms[:, 1, :, :, :],
+                op=ALU.add,
+            )
+
+        def add_pairs(eng, h, cs):
             terms = expd[:, h, cs, :].rearrange("p c (e q l) -> p e c q l", e=2, l=L)
-            nc.vector.tensor_tensor(
+            eng.tensor_tensor(
                 out=pair_sums[:, h, :, :, cs, :].rearrange("p s u c l -> p c (s u) l"),
                 in0=terms[:, 0, :, :, :],
                 in1=terms[:, 1, :, :, :],
                 op=ALU.add,
             )
 
-        add_pairs(0, slice(0, 3))
-        add_pairs(0, slice(3, 4))
-        add_pairs(1, slice(1, 3))
-        add_pairs(1, slice(0, 4, 3))
+        add_pairs(nc.gpsimd, 0, slice(0, 1))
+        add_chunk(nc.gpsimd, 1)
+        add_chunk(nc.vector, 2)
+        add_pairs(nc.vector, 0, slice(3, 4))
+        add_pairs(nc.vector, 1, slice(0, 1))
+        add_pairs(nc.vector, 1, slice(3, 4))
         for u in range(2):
             for s in range(2):
                 nc.tensor.matmul(

@@ -119,9 +119,12 @@ def tile_picked_lsep_none_lo_kernel(tc, xT, w1, offs, out_0, out_1, out_2):
         tops = sb.tile([P, 2, 2, C, L], F32, name="tops", tag="slot2", align_bytes=64)
         logs = sb.tile([P, PACK, V], F32, name="logs")
         result = sb.tile([P, PACK, V], F32, name="result")
-        expd = sb.tile([P, 2, C + 1, D * HV], F32, name="expd")
-        shifted = {c: sb.tile([P, 2, D * HV], F32, name="shifted%d" % c)[:] for c in (2, 3)}
-        shifted[1] = expd[:].rearrange("p h s n -> p (h s) n")[:, C : C + 2, :]
+        expd = {c: sb.tile([P, 2, D * HV], F32, name="expd%d" % c)[:] for c in (1, 2, 3)}
+        shifted = {c: sb.tile([P, 2, D * HV], F32, name="shifted%d" % c, tag="shifted%d" % c)[:] for c in (1, 2, 3)}
+        halves_of_first = {0: sb.tile([P, D * HV], F32, name="first0")[:]}
+
+        def terms_of(c, h):
+            return halves_of_first[h] if c == 0 else expd[c][:, h, :]
 
         def largest(c, hs):
             nc.vector.tensor_reduce(
@@ -142,8 +145,8 @@ def tile_picked_lsep_none_lo_kernel(tc, xT, w1, offs, out_0, out_1, out_2):
                 op=ALU.subtract,
             )
 
-        def exp(c, hs):
-            nc.scalar.activation(expd[:, hs, c, :], shifted[c][:, hs, :], ACT.Exp)
+        def exp(c, h):
+            nc.scalar.activation(terms_of(c, h), shifted[c][:, h, :], ACT.Exp)
 
         one = [slice(0, 1), slice(1, 2)]
 
@@ -162,7 +165,7 @@ def tile_picked_lsep_none_lo_kernel(tc, xT, w1, offs, out_0, out_1, out_2):
 
         def exp_whole(c):
             nc.scalar.activation(
-                expd[:, :, c, :].rearrange("p h (d n) -> p d h n", d=D),
+                expd[c].rearrange("p h (d n) -> p d h n", d=D),
                 shifted[c].rearrange("p h n -> p (h n)").rearrange("p (d h n) -> p d h n", d=D, h=2),
                 ACT.Exp,
             )
@@ -174,19 +177,20 @@ def tile_picked_lsep_none_lo_kernel(tc, xT, w1, offs, out_0, out_1, out_2):
         spill(0, 0)
         spill(0, 1)
         largest(1, both)
-        exp(0, one[0])
+        exp(0, 0)
         sub_whole(1)
         exp_whole(1)
         largest(2, both)
-        exp(0, one[1])
+        halves_of_first[1] = sb.tile([P, D * HV], F32, name="first1", tag="shifted1")[:]
+        exp(0, 1)
         sub_whole(2)
         exp_whole(2)
         largest(3, one[0])
         largest(3, one[1])
         shift(nc.vector, scores(3, 0), 3, 0)
-        exp(3, one[0])
+        exp(3, 0)
         shift(nc.vector, scores(3, 1), 3, 1)
-        exp(3, one[1])
+        exp(3, 1)
 
         top_bank = psum.tile([P, PACK, V], F32, name="top_bank")
         sum_bank = psum.tile([P, PACK, V], F32, name="sum_bank")
@@ -194,10 +198,10 @@ def tile_picked_lsep_none_lo_kernel(tc, xT, w1, offs, out_0, out_1, out_2):
             nc.tensor.transpose(top_bank[:, t, :], tops[:, t // 2, t % 2, :, :].rearrange("p c l -> p (c l)"), ident[:])
 
         pair_sums = sb.tile([P, 2, 2, 2, C, L], F32, name="pair_sums")
-        sums = sb.tile([P, 2, P], F32, name="sums")
+        sums = sb.tile([P, PACK - 1, P], F32, name="sums")
 
         def add_chunk(eng, c):
-            terms = expd[:, :, c, :].rearrange("p h (e q l) -> p e h q l", e=2, l=L)
+            terms = expd[c].rearrange("p h (e q l) -> p e h q l", e=2, l=L)
             eng.tensor_tensor(
                 out=pair_sums[:, :, :, :, c, :].rearrange("p h s u l -> p h (s u) l"),
                 in0=terms[:, 0, :, :, :],
@@ -205,39 +209,38 @@ def tile_picked_lsep_none_lo_kernel(tc, xT, w1, offs, out_0, out_1, out_2):
                 op=ALU.add,
             )
 
-        def add_pairs(eng, h, cs):
-            terms = expd[:, h, cs, :].rearrange("p c (e q l) -> p e c q l", e=2, l=L)
+        def add_half(eng, c, h):
+            terms = terms_of(c, h).rearrange("p (e q l) -> p e q l", e=2, l=L)
             eng.tensor_tensor(
-                out=pair_sums[:, h, :, :, cs, :].rearrange("p s u c l -> p c (s u) l"),
-                in0=terms[:, 0, :, :, :],
-                in1=terms[:, 1, :, :, :],
+                out=pair_sums[:, h, :, :, c, :].rearrange("p s u l -> p (s u) l"),
+                in0=terms[:, 0, :, :],
+                in1=terms[:, 1, :, :],
                 op=ALU.add,
             )
 
-        add_pairs(nc.gpsimd, 0, slice(0, 1))
+        add_half(nc.gpsimd, 0, 0)
         add_chunk(nc.gpsimd, 1)
         add_chunk(nc.vector, 2)
-        add_pairs(nc.vector, 0, slice(3, 4))
-        add_pairs(nc.vector, 1, slice(0, 1))
-        add_pairs(nc.vector, 1, slice(3, 4))
-        for u in range(2):
-            for s in range(2):
-                nc.tensor.matmul(
-                    sum_bank[:, u, :],
-                    lhsT=pair_sums[:, 0, s, u, :, :].rearrange("p c l -> p (c l)"),
-                    rhs=ident[:],
-                    is_transpose=True,
-                    start=(s == 0),
-                    stop=(s == 1),
-                )
-        for u in range(2):
+        add_half(nc.vector, 3, 0)
+        add_half(nc.vector, 0, 1)
+        add_half(nc.vector, 3, 1)
+        for s in range(2):
+            nc.tensor.matmul(
+                sum_bank[:, 0, :],
+                lhsT=pair_sums[:, 0, s, 0, :, :].rearrange("p c l -> p (c l)"),
+                rhs=ident[:],
+                is_transpose=True,
+                start=(s == 0),
+                stop=(s == 1),
+            )
+        for t in range(1, PACK):
             nc.vector.tensor_tensor(
-                out=sums[:, u, :],
-                in0=pair_sums[:, 1, 0, u, :, :].rearrange("p c l -> p (c l)"),
-                in1=pair_sums[:, 1, 1, u, :, :].rearrange("p c l -> p (c l)"),
+                out=sums[:, t - 1, :],
+                in0=pair_sums[:, t // 2, 0, t % 2, :, :].rearrange("p c l -> p (c l)"),
+                in1=pair_sums[:, t // 2, 1, t % 2, :, :].rearrange("p c l -> p (c l)"),
                 op=ALU.add,
             )
-            nc.tensor.transpose(sum_bank[:, 2 + u, :], sums[:, u, :], ident[:])
+            nc.tensor.transpose(sum_bank[:, t, :], sums[:, t - 1, :], ident[:])
         top = top_bank
         QV = HV // 2
         quarters = [slice(q * QV, (q + 1) * QV) for q in range(4)]

from contextlib import ExitStack

import concourse.mybir as mybir
from concourse.masks import make_identity

K, T, S, V, N = 512, 1024, 512, 128, 512
D = S // V
FLOPS = 2 * K * S * N

F32 = mybir.dt.float32
BF16 = mybir.dt.bfloat16
U32 = mybir.dt.uint32
I32 = mybir.dt.int32
U16 = mybir.dt.uint16
U8 = mybir.dt.uint8
FP8X4 = mybir.dt.float8_e4m3fn_x4
ALU = mybir.AluOpType
ACT = mybir.ActivationFunctionType
AX = mybir.AxisListType

P = 128
PACK = 4


def tile_picked_lsep_none_lo_kernel(tc, xT, w1, offs, out_0, out_1, out_2):
    nc = tc.nc
    with ExitStack() as ctx:
        sb = ctx.enter_context(tc.tile_pool(name="sb", bufs=1))
        psum = ctx.enter_context(tc.psum_pool(name="psum", bufs=1))

        offsets = sb.tile([P, S // 16], U16, name="offsets")
        warm = sb.tile([P, 8], F32, name="warm")
        warm_out = sb.tile([P, 8], F32, name="warm_out")
        nc.vector.memset(warm[:], 0.0)
        nc.scalar.activation(warm_out[:], warm[:], ACT.Exp)

        x_rows = xT.rearrange("(p j) t -> p j t", j=PACK)
        w_rows = w1.rearrange("(p j) m -> p j m", j=PACK)
        planes = [sb.tile([P, T], F32, name="plane%d" % j) for j in range(PACK)]
        CUT = 5 * T // 8
        nc.scalar.dma_start(out=planes[0][:, :CUT], in_=x_rows[:, 0, :CUT])
        nc.sync.dma_start(offsets[:], offs)
        nc.sync.dma_start(out=planes[0][:, CUT:], in_=x_rows[:, 0, CUT:])
        for j in range(1, PACK):
            nc.sync.dma_start(out=planes[j][:], in_=x_rows[:, j, :])
        C = N // P
        L = P // PACK
        w_raw = [sb.tile([P, PACK, P], F32, name="w_raw%d" % c) for c in range(C)]
        for c in range(C):
            nc.sync.dma_start(out=w_raw[c][:], in_=w_rows[:, :, c * P : (c + 1) * P])
        ident = sb.tile([P, P], F32, name="ident")
        make_identity(nc, ident[:])

        HS = S // 2
        x_grouped = [sb.tile([P, HS * PACK], BF16, name="x_grouped%d" % h, align_bytes=64) for h in range(2)]
        picked = [sb.tile([P, 2, HS], BF16, name="picked%d" % a) for a in range(2)]
        slots = [g[:].rearrange("p (n j) -> p n j", j=PACK) for g in x_grouped]
        for j in range(PACK):
            nc.scalar.activation(picked[j // 2][:, j % 2, :], planes[j][:].indirect(offsets[:, HS // 16 :]), ACT.Copy)
            nc.vector.tensor_copy(slots[0][:, :, j], planes[j][:].indirect(offsets[:, : HS // 16]))
            if j % 2:
                nc.vector.tensor_copy(slots[1][:, :, j - 1 : j + 1], picked[j // 2][:].rearrange("p e n -> p n e"))

        w_grouped = [
            sb.tile([P, PACK, L, PACK], BF16, name="w_grouped%d" % c, tag="slot%d" % c, align_bytes=64) for c in range(C)
        ]
        for c in range(C):
            nc.scalar.copy(
                out=w_grouped[c][:].rearrange("p t l j -> p l j t"),
                in_=w_raw[c][:].rearrange("p j (l t) -> p l j t", t=PACK),
            )

        x_codes = {0: sb.tile([P, HS], U32, name="x_codes0", align_bytes=64)}
        x_scales = sb.tile([P, S], U8, name="x_scales", align_bytes=64)
        w_codes = [sb.tile([P, P], U32, name="w_codes%d" % c, align_bytes=64) for c in range(C - 1)]
        w_codes.append(w_codes[0])
        w_scales = [sb.tile([P, P], U8, name="w_scales%d" % c, align_bytes=64) for c in range(C)]
        banks = [psum.tile([P, S], F32, name="bank%d" % c) for c in range(C)]

        def quantise_x(h, lo, hi):
            nc.vector.quantize_mx(
                out=x_codes[h][:, lo:hi].bitcast(FP8X4),
                scales=x_scales[:, h * HS + lo : h * HS + hi],
                in_=x_grouped[h][:, lo * PACK : hi * PACK],
            )

        def quantise_w(c):
            nc.vector.quantize_mx(
                out=w_codes[c][:].bitcast(FP8X4),
                scales=w_scales[c][:],
                in_=w_grouped[c][:].rearrange("p t l j -> p (t l j)"),
            )

        def products(c):
            for d in range(D):
                nc.tensor.matmul_mx(
                    out=banks[c][:, d * V : (d + 1) * V],
                    lhsT=x_codes[d // 2][:, (d % 2) * V : (d % 2 + 1) * V].bitcast(FP8X4),
                    lhsT_scale=x_scales[:, d * V : (d + 1) * V],
                    rhs=w_codes[c][:].bitcast(FP8X4),
                    rhs_scale=w_scales[c][:],
                    start=True,
                    stop=True,
                )

        quantise_x(0, 0, HS)
        quantise_w(0)
        x_codes[1] = sb.tile([P, HS], U32, name="x_codes1", tag="slot0", align_bytes=64)
        quantise_x(1, 0, V)
        quantise_x(1, V, HS)
        products(0)
        for c in range(1, C - 1):
            quantise_w(c)
            products(c)

        HV = V // 2
        halves = [slice(0, HV), slice(HV, V)]
        both = slice(0, 2)
        tops = sb.tile([P, 2, 2, C, L], F32, name="tops", tag="slot2", align_bytes=64)
        logs = sb.tile([P, PACK, V], F32, name="logs")
        result = sb.tile([P, PACK, V], F32, name="result")
        expd = {c: sb.tile([P, 2, D * HV], F32, name="expd%d" % c)[:] for c in (1, 2, 3)}
        shifted = {c: sb.tile([P, 2, D * HV], F32, name="shifted%d" % c, tag="shifted%d" % c)[:] for c in (1, 2, 3)}
        halves_of_first = {0: sb.tile([P, D * HV], F32, name="first0")[:]}

        def terms_of(c, h):
            return halves_of_first[h] if c == 0 else expd[c][:, h, :]

        def largest(c, hs):
            nc.vector.tensor_reduce(
                out=tops[:, hs, :, c, :].rearrange("p h u l -> p (h u) l"),
                in_=banks[c][:].rearrange("p (d t l) -> p t l d", d=D, l=L)[:, 2 * hs.start : 2 * hs.stop, :, :],
                axis=AX.X,
                op=ALU.max,
            )

        def scores(c, h):
            return banks[c][:].rearrange("p (d h u l) -> p h d u l", d=D, h=2, u=2)[:, h, :, :, :]

        def shift(eng, src, c, h):
            eng.tensor_tensor(
                out=shifted[c][:, h, :].rearrange("p (d u l) -> p d u l", d=D, u=2),
                in0=src,
                in1=tops[:, h, :, c, :].unsqueeze(1).to_broadcast([P, D, 2, L]),
                op=ALU.subtract,
            )

        def exp(c, h):
            nc.scalar.activation(terms_of(c, h), shifted[c][:, h, :], ACT.Exp)

        one = [slice(0, 1), slice(1, 2)]

        def spill(c, h):
            spilled = sb.tile([P, D, 2, L], F32, name="spilled%d%d" % (c, h))
            nc.scalar.copy(out=spilled[:], in_=scores(c, h))
            shift(nc.gpsimd, spilled[:], c, h)

        def sub_whole(c):
            nc.vector.tensor_tensor(
                out=shifted[c].rearrange("p h (t l) -> p (h t) l", l=L).rearrange("p (d t) l -> p d t l", d=D),
                in0=banks[c][:].rearrange("p (d t l) -> p d t l", d=D, l=L),
                in1=tops[:, :, :, c, :].rearrange("p h u l -> p (h u) l").unsqueeze(1).to_broadcast([P, D, PACK, L]),
                op=ALU.subtract,
            )

        def exp_whole(c):
            nc.scalar.activation(
                expd[c].rearrange("p h (d n) -> p d h n", d=D),
                shifted[c].rearrange("p h n -> p (h n)").rearrange("p (d h n) -> p d h n", d=D, h=2),
                ACT.Exp,
            )

        largest(0, both)
        quantise_w(3)
        products(3)
        shifted[0] = sb.tile([P, 2, D * HV], F32, name="shifted0", tag="slot3", align_bytes=64)[:]
        spill(0, 0)
        spill(0, 1)
        largest(1, both)
        exp(0, 0)
        sub_whole(1)
        exp_whole(1)
        largest(2, both)
        halves_of_first[1] = sb.tile([P, D * HV], F32, name="first1", tag="shifted1")[:]
        exp(0, 1)
        sub_whole(2)
        exp_whole(2)
        largest(3, one[0])
        largest(3, one[1])
        shift(nc.vector, scores(3, 0), 3, 0)
        exp(3, 0)
        shift(nc.vector, scores(3, 1), 3, 1)
        exp(3, 1)

        top_bank = psum.tile([P, PACK, V], F32, name="top_bank")
        sum_bank = psum.tile([P, PACK, V], F32, name="sum_bank")
        for t in range(PACK):
            nc.tensor.transpose(top_bank[:, t, :], tops[:, t // 2, t % 2, :, :].rearrange("p c l -> p (c l)"), ident[:])

        pair_sums = sb.tile([P, 2, 2, 2, C, L], F32, name="pair_sums")
        sums = sb.tile([P, PACK - 1, P], F32, name="sums")

        def add_chunk(eng, c):
            terms = expd[c].rearrange("p h (e q l) -> p e h q l", e=2, l=L)
            eng.tensor_tensor(
                out=pair_sums[:, :, :, :, c, :].rearrange("p h s u l -> p h (s u) l"),
                in0=terms[:, 0, :, :, :],
                in1=terms[:, 1, :, :, :],
                op=ALU.add,
            )

        def add_half(eng, c, h):
            terms = terms_of(c, h).rearrange("p (e q l) -> p e q l", e=2, l=L)
            eng.tensor_tensor(
                out=pair_sums[:, h, :, :, c, :].rearrange("p s u l -> p (s u) l"),
                in0=terms[:, 0, :, :],
                in1=terms[:, 1, :, :],
                op=ALU.add,
            )

        add_half(nc.gpsimd, 0, 0)
        add_chunk(nc.gpsimd, 1)
        add_chunk(nc.vector, 2)
        add_half(nc.vector, 3, 0)
        add_half(nc.vector, 0, 1)
        add_half(nc.vector, 3, 1)
        for s in range(2):
            nc.tensor.matmul(
                sum_bank[:, 0, :],
                lhsT=pair_sums[:, 0, s, 0, :, :].rearrange("p c l -> p (c l)"),
                rhs=ident[:],
                is_transpose=True,
                start=(s == 0),
                stop=(s == 1),
            )
        for t in range(1, PACK):
            nc.vector.tensor_tensor(
                out=sums[:, t - 1, :],
                in0=pair_sums[:, t // 2, 0, t % 2, :, :].rearrange("p c l -> p (c l)"),
                in1=pair_sums[:, t // 2, 1, t % 2, :, :].rearrange("p c l -> p (c l)"),
                op=ALU.add,
            )
            nc.tensor.transpose(sum_bank[:, t, :], sums[:, t - 1, :], ident[:])
        top = top_bank
        QV = HV // 2
        quarters = [slice(q * QV, (q + 1) * QV) for q in range(4)]
        y_grouped = [sb.tile([P, HV * PACK], BF16, name="y_grouped%d" % h, align_bytes=64) for h in range(2)]
        y_codes = sb.tile([P, V], U32, name="y_codes", align_bytes=64)
        y_scales = sb.tile([P, V], U8, name="y_scales", align_bytes=64)

        def by_lines(rows):
            return rows.rearrange("p t (c i) -> p c t i", i=4)

        def grouped(q):
            part = y_grouped[q // 2][:, (q % 2) * QV * PACK : (q % 2 + 1) * QV * PACK]
            return part.rearrange("p (c i t) -> p c t i", i=4, t=PACK)

        for q, vs in enumerate(quarters):
            nc.scalar.activation(logs[:, :, vs], sum_bank[:, :, vs], ACT.Ln)
        for q, vs in enumerate(quarters):
            nc.vector.tensor_tensor(out=result[:, :, vs], in0=logs[:, :, vs], in1=top[:, :, vs], op=ALU.add)
        nc.sync.dma_start(out=out_0.rearrange("(p t) v -> p t v", t=PACK), in_=result[:])
        for q in (0, 1):
            nc.scalar.copy(out=grouped(q), in_=by_lines(result[:, :, quarters[q]]))
        vs = quarters[3]
        nc.vector.tensor_tensor(out=grouped(3), in0=by_lines(logs[:, :, vs]), in1=by_lines(top[:, :, vs]), op=ALU.add)
        nc.vector.tensor_copy(out=grouped(2), in_=by_lines(result[:, :, quarters[2]]))
        for h, vs in enumerate(halves):
            nc.vector.quantize_mx(out=y_codes[:, vs].bitcast(FP8X4), scales=y_scales[:, vs], in_=y_grouped[h][:])
        nc.scalar.dma_start(
            out=out_1.rearrange("z l c r -> (z l) (c r)").bitcast(I32), in_=y_codes[:].bitcast(I32)
        )
        scale_rows = out_2.rearrange("z q c -> (z q) c").bitcast(I32)
        for q in range(4):
            eng = nc.scalar if q == 1 else nc.sync
            eng.dma_start(out=scale_rows[4 * q : 4 * q + 4, :], in_=y_scales[32 * q : 32 * q + 4, :].bitcast(I32))
